import numpy as np, ml_dtypes
CORES = [242,247,114,119]
N = 4
TK, LAY = 512, 2
def setup_inputs(rng):
    return {"x": rng.standard_normal((N, 128, TK), dtype=np.float32).astype(ml_dtypes.bfloat16), "wu": (rng.standard_normal((N, 128, LAY * 256), dtype=np.float32) / 16).astype(ml_dtypes.bfloat16), "wd": (rng.standard_normal((N, 128, 256), dtype=np.float32) / 16).astype(ml_dtypes.bfloat16)}
def setup_inputs_big(rng):
    d = setup_inputs(rng)
    for k in ("x",): d[k] = (d[k].astype(np.float32) * 1048576.0).astype(d[k].dtype)
    return d
def setup_inputs_small(rng):
    d = setup_inputs(rng)
    for k in ("x",): d[k] = (d[k].astype(np.float32) * (1 / 1048576.0)).astype(d[k].dtype)
    return d
def setup_inputs_apart(rng):
    d = setup_inputs(rng)
    f = (10.0 ** rng.permutation(np.linspace(-1.5, 1.5, N))).astype(np.float32).reshape(N, 1, 1)
    for k in ("x",): d[k] = (d[k].astype(np.float32) * f).astype(d[k].dtype)
    return d
def reference(x, wu, wd):
    X, WU, WD = x.astype(np.float64), wu.astype(np.float64), wd.astype(np.float64)
    s = list(X)
    for l in range(LAY):
        for q in range(0, N, 2 << l):
            p = q + (1 << l)
            s[q] = np.maximum(WU[q][:, 256 * l:256 * l + 128].T @ s[q] + WU[q][:, 256 * l + 128:256 * l + 256].T @ s[p], 0.0)
    for l in range(LAY - 1, -1, -1):
        for q in range(0, N, 2 << l):
            p = q + (1 << l)
            s[p] = np.maximum(WD[p][:, 0:128].T @ s[p] + WD[p][:, 128:256].T @ s[q], 0.0)
    return {"y": np.stack(s).astype(ml_dtypes.bfloat16)}

@@ -1,0 +1,169 @@
+from concourse.bass import DstId, RemoteDMATransfer
+from concourse.mybir import AluOpType
+
+TK = 512
+H = 2
+CW = TK // H
+
+SCRATCH = {
+    "a": ("sbuf", [128, TK + 256], "bfloat16"),
+    "xp": ("sbuf", [128, TK], "bfloat16"),
+    "w1": ("sbuf", [128, 256], "bfloat16"),
+    "wd2": ("sbuf", [128, 256], "bfloat16"),
+    "wo": ("sbuf", [128, 256], "bfloat16"),
+    "so": ("sbuf", [128, TK], "bfloat16"),
+    "sx": ("sbuf", [128, TK], "bfloat16"),
+    "o1": ("sbuf", [128, TK], "bfloat16"),
+    "o2": ("sbuf", [128, TK], "bfloat16"),
+    "o3": ("sbuf", [128, TK], "bfloat16"),
+    "zero": ("sbuf", [128, CW], "bfloat16"),
+}
+for _s in range(4):
+    for _h in range(H):
+        SCRATCH["p%d%d" % (_s, _h)] = ("psum", [128, 512], "float32")
+
+SEMAPHORES = ["lda", "ldx", "ldw", "ldd", "arrA", "arrX", "arrW", "arrD", "arrS", "zs", "sent", "st"]
+SEMAPHORES += ["m%d%d" % (s, h) for s in range(4) for h in range(H)]
+SEMAPHORES += ["v%d%d" % (s, h) for s in range(4) for h in range(H)]
+
+
+def count(mask):
+    return bin(mask).count("1")
+
+
+def lanes(topo, src, cores, partner):
+    lo = topo.mask(src, partner)
+    for d in cores:
+        if d != src:
+            lo &= topo.mask(src, d)
+    hi = topo.mask(src, partner) & ~lo
+    return lo, (hi if hi else lo)
+
+
+def rank_program(g, core, T, topo):
+    rank = T.rank_of(core)
+    if rank is None:
+        return
+    S, cores = T.sem, T.cores
+    te, ve = g.tensor, g.vector
+    even = rank % 2 == 0
+    top = rank < 2
+    mate = cores[rank ^ 1]
+    far = cores[3 - rank]
+    lo, hi = lanes(topo, core, cores, mate)
+    mate_lo, mate_hi = lanes(topo, mate, cores, core)
+    far_lo = lanes(topo, far, cores, cores[(3 - rank) ^ 1])[0]
+    r0_lo, r0_hi = lanes(topo, cores[0], cores, cores[1])
+    cols = [slice(h * CW, (h + 1) * CW) for h in range(H)]
+    sent = [0]
+
+    def send(dst, buf_out, buf_in, sem, mask):
+        rid, pid = topo.addr(dst, core)
+        g.remote_dma(out_ap=buf_out, in_ap=buf_in, remote_sem=sem, local_sem=S.sent, pid=pid, routing_id=rid,
+                     dma_engine_mask=mask)
+        sent[0] += count(mask)
+
+    def mm(stage, h, w, rhs, start, stop):
+        i = te.matmul(T["p%d%d" % (stage, h)][:, 0:CW], w, rhs[:, cols[h]], start, stop)
+        if stop:
+            i.then_inc(S["m%d%d" % (stage, h)], 1)
+
+    if even:
+        g.sync.dma_start(T.a[:, 0:TK], T.x[:, :]).then_inc(S.lda, 16)
+        g.scalar.dma_start(T.a[:, TK:TK + 256], T.wu[:, 0:256]).then_inc(S.lda, 16)
+        if top:
+            g.scalar.dma_start(T.w1[:, :], T.wu[:, 256:512]).then_inc(S.ldw, 16)
+        else:
+            g.scalar.dma_start(T.wd2[:, :], T.wd[:, :]).then_inc(S.ldd, 16)
+    else:
+        g.sync.dma_start(T.xp[:, :], T.x[:, :]).then_inc(S.ldx, 16)
+        g.scalar.dma_start(T.wo[:, :], T.wd[:, :]).then_inc(S.ldd, 16)
+
+    if even:
+        g.wait_ge(S.lda, 32)
+        send(mate, T.a[:, :], T.a[:, :], S.arrA, hi)
+        if top:
+            g.wait_ge(S.ldw, 16)
+            offchip = [cores[2], cores[3]]
+            ids = [topo.addr(d, core) for d in offchip]
+            rid1, pid1 = topo.addr(mate, core)
+            g.remote_dma_fused([
+                RemoteDMATransfer(dst_ids=[DstId(rid=r, pnc=p) for r, p in ids], dma_engine_mask=lo, remote_sem=S.arrW,
+                                  srcs=[T.w1[:, :]], dsts=[T.w1[:, :] for _ in ids]),
+                RemoteDMATransfer(dst_ids=[DstId(rid=rid1, pnc=pid1)], dma_engine_mask=hi, remote_sem=S.arrW,
+                                  srcs=[T.w1[:, :]], dsts=[T.w1[:, :]]),
+            ], local_sem=S.sent)
+            sent[0] += count(lo) + count(hi)
+        else:
+            g.wait_ge(S.ldd, 16)
+            send(mate, T.wd2[:, :], T.wd2[:, :], S.arrD, lo)
+    else:
+        g.wait_ge(S.ldx, 16)
+        send(mate, T.xp[:, :], T.xp[:, :], S.arrX, lo)
+    for h in range(H):
+        g.wait_ge(S["v0%d" % h], 1)
+    send(far, T.sx[:, :], T.so[:, :], S.arrS, lo)
+
+    U0, V0 = T.a[:, TK:TK + 128], T.a[:, TK + 128:TK + 256]
+    U1, V1 = T.w1[:, 0:128], T.w1[:, 128:256]
+    if even:
+        te.wait_ge(S.lda, 32)
+        for h in range(H):
+            mm(0, h, U0, T.a, True, False)
+        te.wait_ge(S.arrX, count(mate_lo))
+        for h in range(H):
+            mm(0, h, V0, T.xp, False, True)
+    else:
+        te.wait_ge(S.ldx, 16)
+        te.wait_ge(S.ldd, 16)
+        for h in range(H):
+            mm(3, h, T.wo[:, 0:128], T.xp, True, False)
+        te.wait_ge(S.arrA, count(mate_hi))
+        for h in range(H):
+            mm(0, h, U0, T.a, True, False)
+            mm(0, h, V0, T.xp, False, True)
+    if rank == 0:
+        te.wait_ge(S.ldw, 16)
+    else:
+        te.wait_ge(S.arrW, count(r0_hi if top else r0_lo))
+    for h in range(H):
+        te.wait_ge(S["v0%d" % h], 1)
+        mm(1, h, U1 if top else V1, T.so, True, False)
+    if not top:
+        if even:
+            te.wait_ge(S.ldd, 16)
+        else:
+            te.wait_ge(S.arrD, count(mate_lo))
+        for h in range(H):
+            mm(2, h, T.wd2[:, 0:128], T.so, True, False)
+    te.wait_ge(S.arrS, count(far_lo))
+    for h in range(H):
+        mm(1, h, V1 if top else U1, T.sx, False, True)
+    stages = [0, 1]
+    if not top:
+        stages.append(2)
+        for h in range(H):
+            te.wait_ge(S["v1%d" % h], 1)
+            mm(2, h, T.wd2[:, 128:256], T.o1, False, True)
+    if not even:
+        prev = stages[-1]
+        stages.append(3)
+        for h in range(H):
+            te.wait_ge(S["v%d%d" % (prev, h)], 1)
+            mm(3, h, T.wo[:, 128:256], T["o%d" % prev], False, True)
+
+    ve.memset(T.zero[:, :], 0.0).then_inc(S.zs, 1)
+    ve.wait_ge(S.zs, 1)
+    for s in stages:
+        out = T.so if s == 0 else T["o%d" % s]
+        for h in range(H):
+            ve.wait_ge(S["m%d%d" % (s, h)], 1)
+            ve.tensor_tensor(out[:, cols[h]], T["p%d%d" % (s, h)][:, 0:CW], T.zero[:, :],
+                             AluOpType.max).then_inc(S["v%d%d" % (s, h)], 1)
+
+    last = stages[-1]
+    for h in range(H):
+        g.sync.wait_ge(S["v%d%d" % (last, h)], 1)
+    g.sync.dma_start(T.y[:, :], T["o%d" % last][:, :]).then_inc(S.st, 16)
+    g.sync.wait_ge(S.st, 16)
+    g.wait_ge(S.sent, sent[0])

@@ -1,30 +1,31 @@
 from concourse.bass import DstId, RemoteDMATransfer
-from concourse.mybir import AluOpType
+from concourse.mybir import AluOpType, ActivationFunctionType
 
 TK = 512
-H = 2
-CW = TK // H
+CW = TK // 2
 
 SCRATCH = {
-    "a": ("sbuf", [128, TK + 256], "bfloat16"),
+    "xq": ("sbuf", [128, TK], "bfloat16"),
+    "w0": ("sbuf", [128, 256], "bfloat16"),
     "xp": ("sbuf", [128, TK], "bfloat16"),
     "w1": ("sbuf", [128, 256], "bfloat16"),
     "wd2": ("sbuf", [128, 256], "bfloat16"),
     "wo": ("sbuf", [128, 256], "bfloat16"),
-    "so": ("sbuf", [128, TK], "bfloat16"),
-    "sx": ("sbuf", [128, TK], "bfloat16"),
+    "so0": ("sbuf", [128, CW], "bfloat16"),
+    "so1": ("sbuf", [128, CW], "bfloat16"),
+    "sx0": ("sbuf", [128, CW], "bfloat16"),
+    "sx1": ("sbuf", [128, CW], "bfloat16"),
     "o1": ("sbuf", [128, TK], "bfloat16"),
     "o2": ("sbuf", [128, TK], "bfloat16"),
     "o3": ("sbuf", [128, TK], "bfloat16"),
     "zero": ("sbuf", [128, CW], "bfloat16"),
 }
-for _s in range(4):
-    for _h in range(H):
-        SCRATCH["p%d%d" % (_s, _h)] = ("psum", [128, 512], "float32")
+for _b in range(8):
+    SCRATCH["b%d" % _b] = ("psum", [128, 512], "float32")
 
-SEMAPHORES = ["lda", "ldx", "ldw", "ldd", "arrA", "arrX", "arrW", "arrD", "arrS", "zs", "sent", "st"]
-SEMAPHORES += ["m%d%d" % (s, h) for s in range(4) for h in range(H)]
-SEMAPHORES += ["v%d%d" % (s, h) for s in range(4) for h in range(H)]
+SEMAPHORES = ["ldx", "ldu", "ldw", "ldd", "arrA", "arrU", "arrX", "arrW", "arrD", "arrS0", "arrS1", "zs", "sent", "st"]
+SEMAPHORES += ["m%d%d" % (s, k) for s in range(4) for k in range(4)]
+SEMAPHORES += ["v%d%d" % (s, k) for s in range(4) for k in range(4)]
 
 
 def count(mask):
@@ -45,17 +46,37 @@ def rank_program(g, core, T, topo):
     if rank is None:
         return
     S, cores = T.sem, T.cores
-    te, ve = g.tensor, g.vector
+    te, ve, ac = g.tensor, g.vector, g.scalar
     even = rank % 2 == 0
     top = rank < 2
     mate = cores[rank ^ 1]
-    far = cores[3 - rank]
+    far_even, far_odd = (cores[2], cores[3]) if top else (cores[0], cores[1])
     lo, hi = lanes(topo, core, cores, mate)
     mate_lo, mate_hi = lanes(topo, mate, cores, core)
-    far_lo = lanes(topo, far, cores, cores[(3 - rank) ^ 1])[0]
     r0_lo, r0_hi = lanes(topo, cores[0], cores, cores[1])
-    cols = [slice(h * CW, (h + 1) * CW) for h in range(H)]
+    s_in = [count(lanes(topo, far_even, cores, far_odd)[0]), count(lanes(topo, far_odd, cores, far_even)[0])]
+    w1_in = {1: count(r0_hi), 3: count(r0_lo), 2: count(mate_lo)}.get(rank, 0)
     sent = [0]
+
+    hs = 0 if even else 1
+    b0, b1 = hs * CW, (1 - hs) * CW
+    stages = [0, 1] + ([] if top else [2]) + ([] if even else [3])
+    last = stages[-1]
+    P = {0: [(b0, b0 + 128, 0, "v"), (b0 + 128, b0 + 192, 1, "s"), (b0 + 192, b0 + 256, 2, "v"), (b1, b1 + 256, 3, "s")]}
+    mid_banks = [(0, 3), (1, 2)]
+    for s in stages[1:-1]:
+        ba, bb = mid_banks.pop(0)
+        P[s] = [(0, 256, ba, "v"), (256, 512, bb, "v")]
+    P[last] = [(0, 256, 4, "s"), (256, 384, 5, "v"), (384, 448, 6, "v"), (448, 512, 7, "s")]
+
+    def halves(name):
+        return lambda c0, c1: T["%s%d" % (name, c0 // CW)][:, c0 % CW:c0 % CW + (c1 - c0)]
+
+    def whole(name):
+        return lambda c0, c1: T[name][:, c0:c1]
+
+    def outbuf(s):
+        return halves("so") if s == 0 else whole("o%d" % s)
 
     def send(dst, buf_out, buf_in, sem, mask):
         rid, pid = topo.addr(dst, core)
@@ -63,107 +84,123 @@ def rank_program(g, core, T, topo):
                      dma_engine_mask=mask)
         sent[0] += count(mask)
 
-    def mm(stage, h, w, rhs, start, stop):
-        i = te.matmul(T["p%d%d" % (stage, h)][:, 0:CW], w, rhs[:, cols[h]], start, stop)
-        if stop:
-            i.then_inc(S["m%d%d" % (stage, h)], 1)
+    def group(s, w, rhs, first, before=None):
+        for k, (c0, c1, bank, _) in enumerate(P[s]):
+            if before:
+                before(c0, c1)
+            i = te.matmul(T["b%d" % bank][:, 0:c1 - c0], w, rhs(c0, c1), first, not first)
+            if not first:
+                i.then_inc(S["m%d%d" % (s, k)], 1)
+
+    def after(s):
+        def f(c0, c1):
+            for k, (d0, d1, _, _) in enumerate(P[s]):
+                if d0 < c1 and c0 < d1:
+                    te.wait_ge(S["v%d%d" % (s, k)], 1)
+        return f
 
     if even:
-        g.sync.dma_start(T.a[:, 0:TK], T.x[:, :]).then_inc(S.lda, 16)
-        g.scalar.dma_start(T.a[:, TK:TK + 256], T.wu[:, 0:256]).then_inc(S.lda, 16)
+        g.sync.dma_start(T.xq[:, :], T.x[:, :]).then_inc(S.ldx, 16)
+        g.scalar.dma_start(T.w0[:, :], T.wu[:, 0:256]).then_inc(S.ldu, 16)
         if top:
             g.scalar.dma_start(T.w1[:, :], T.wu[:, 256:512]).then_inc(S.ldw, 16)
         else:
             g.scalar.dma_start(T.wd2[:, :], T.wd[:, :]).then_inc(S.ldd, 16)
     else:
         g.sync.dma_start(T.xp[:, :], T.x[:, :]).then_inc(S.ldx, 16)
+        g.scalar.wait_ge(S.ldx, 16)
         g.scalar.dma_start(T.wo[:, :], T.wd[:, :]).then_inc(S.ldd, 16)
 
     if even:
-        g.wait_ge(S.lda, 32)
-        send(mate, T.a[:, :], T.a[:, :], S.arrA, hi)
+        g.wait_ge(S.ldu, 16)
+        send(mate, T.w0[:, :], T.w0[:, :], S.arrU, lo)
+        g.wait_ge(S.ldx, 16)
+        send(mate, T.xq[:, :], T.xq[:, :], S.arrA, hi)
         if top:
             g.wait_ge(S.ldw, 16)
-            offchip = [cores[2], cores[3]]
-            ids = [topo.addr(d, core) for d in offchip]
+            rid3, pid3 = topo.addr(cores[3], core)
             rid1, pid1 = topo.addr(mate, core)
             g.remote_dma_fused([
-                RemoteDMATransfer(dst_ids=[DstId(rid=r, pnc=p) for r, p in ids], dma_engine_mask=lo, remote_sem=S.arrW,
-                                  srcs=[T.w1[:, :]], dsts=[T.w1[:, :] for _ in ids]),
+                RemoteDMATransfer(dst_ids=[DstId(rid=rid3, pnc=pid3)], dma_engine_mask=lo, remote_sem=S.arrW,
+                                  srcs=[T.w1[:, :]], dsts=[T.w1[:, :]]),
                 RemoteDMATransfer(dst_ids=[DstId(rid=rid1, pnc=pid1)], dma_engine_mask=hi, remote_sem=S.arrW,
                                   srcs=[T.w1[:, :]], dsts=[T.w1[:, :]]),
             ], local_sem=S.sent)
             sent[0] += count(lo) + count(hi)
         else:
             g.wait_ge(S.ldd, 16)
-            send(mate, T.wd2[:, :], T.wd2[:, :], S.arrD, lo)
+            send(mate, T.wd2[:, :], T.wd2[:, :], S.arrD, hi)
     else:
         g.wait_ge(S.ldx, 16)
         send(mate, T.xp[:, :], T.xp[:, :], S.arrX, lo)
-    for h in range(H):
-        g.wait_ge(S["v0%d" % h], 1)
-    send(far, T.sx[:, :], T.so[:, :], S.arrS, lo)
+        if not top:
+            g.wait_ge(S.arrW, w1_in)
+            send(mate, T.w1[:, :], T.w1[:, :], S.arrW, lo)
+    for k in range(3):
+        g.wait_ge(S["v0%d" % k], 1)
+    for dst in (far_odd, far_even):
+        send(dst, T["sx%d" % hs][:, :], T["so%d" % hs][:, :], S["arrS%d" % hs], lo)
 
-    U0, V0 = T.a[:, TK:TK + 128], T.a[:, TK + 128:TK + 256]
+    U0, V0 = T.w0[:, 0:128], T.w0[:, 128:256]
     U1, V1 = T.w1[:, 0:128], T.w1[:, 128:256]
+    te.wait_ge(S.ldx, 16)
     if even:
-        te.wait_ge(S.lda, 32)
-        for h in range(H):
-            mm(0, h, U0, T.a, True, False)
+        te.wait_ge(S.ldu, 16)
+        group(0, U0, whole("xq"), True)
         te.wait_ge(S.arrX, count(mate_lo))
-        for h in range(H):
-            mm(0, h, V0, T.xp, False, True)
+        group(0, V0, whole("xp"), False)
     else:
-        te.wait_ge(S.ldx, 16)
-        te.wait_ge(S.ldd, 16)
-        for h in range(H):
-            mm(3, h, T.wo[:, 0:128], T.xp, True, False)
+        te.wait_ge(S.arrU, count(mate_lo))
+        group(0, V0, whole("xp"), True)
         te.wait_ge(S.arrA, count(mate_hi))
-        for h in range(H):
-            mm(0, h, U0, T.a, True, False)
-            mm(0, h, V0, T.xp, False, True)
-    if rank == 0:
-        te.wait_ge(S.ldw, 16)
-    else:
-        te.wait_ge(S.arrW, count(r0_hi if top else r0_lo))
-    for h in range(H):
-        te.wait_ge(S["v0%d" % h], 1)
-        mm(1, h, U1 if top else V1, T.so, True, False)
-    if not top:
+        group(0, U0, whole("xq"), False)
+        te.wait_ge(S.ldd, 16)
+        group(3, T.wo[:, 0:128], whole("xp"), True)
+    after(0)(0, TK)
+
+    def open1():
+        if rank == 0:
+            te.wait_ge(S.ldw, 16)
+        else:
+            te.wait_ge(S.arrW, w1_in)
+        group(1, U1 if top else V1, halves("so"), True)
+
+    def open2():
         if even:
             te.wait_ge(S.ldd, 16)
         else:
-            te.wait_ge(S.arrD, count(mate_lo))
-        for h in range(H):
-            mm(2, h, T.wd2[:, 0:128], T.so, True, False)
-    te.wait_ge(S.arrS, count(far_lo))
-    for h in range(H):
-        mm(1, h, V1 if top else U1, T.sx, False, True)
-    stages = [0, 1]
+            te.wait_ge(S.arrD, count(mate_hi))
+        group(2, T.wd2[:, 0:128], halves("so"), True)
+
+    if top:
+        open1()
+    elif even:
+        open2()
+        open1()
+    else:
+        open1()
+        open2()
+    group(1, V1 if top else U1, halves("sx"), False, lambda c0, c1: te.wait_ge(S["arrS%d" % (c0 // CW)], s_in[c0 // CW]))
     if not top:
-        stages.append(2)
-        for h in range(H):
-            te.wait_ge(S["v1%d" % h], 1)
-            mm(2, h, T.wd2[:, 128:256], T.o1, False, True)
+        group(2, T.wd2[:, 128:256], whole("o1"), False, after(1))
     if not even:
-        prev = stages[-1]
-        stages.append(3)
-        for h in range(H):
-            te.wait_ge(S["v%d%d" % (prev, h)], 1)
-            mm(3, h, T.wo[:, 128:256], T["o%d" % prev], False, True)
+        prev = stages[-2]
+        group(3, T.wo[:, 128:256], whole("o%d" % prev), False, after(prev))
 
     ve.memset(T.zero[:, :], 0.0).then_inc(S.zs, 1)
     ve.wait_ge(S.zs, 1)
     for s in stages:
-        out = T.so if s == 0 else T["o%d" % s]
-        for h in range(H):
-            ve.wait_ge(S["m%d%d" % (s, h)], 1)
-            ve.tensor_tensor(out[:, cols[h]], T["p%d%d" % (s, h)][:, 0:CW], T.zero[:, :],
-                             AluOpType.max).then_inc(S["v%d%d" % (s, h)], 1)
+        for k, (c0, c1, bank, eng) in enumerate(P[s]):
+            acc, out = T["b%d" % bank][:, 0:c1 - c0], outbuf(s)(c0, c1)
+            if eng == "v":
+                ve.wait_ge(S["m%d%d" % (s, k)], 1)
+                ve.tensor_tensor(out, acc, T.zero[:, 0:c1 - c0], AluOpType.max).then_inc(S["v%d%d" % (s, k)], 1)
+            else:
+                ac.wait_ge(S["m%d%d" % (s, k)], 1)
+                ac.activation(out, acc, ActivationFunctionType.Relu).then_inc(S["v%d%d" % (s, k)], 1)
 
-    last = stages[-1]
-    for h in range(H):
-        g.sync.wait_ge(S["v%d%d" % (last, h)], 1)
+    for k in range(len(P[last])):
+        g.sync.wait_ge(S["v%d%d" % (last, k)], 1)
     g.sync.dma_start(T.y[:, :], T["o%d" % last][:, :]).then_inc(S.st, 16)
     g.sync.wait_ge(S.st, 16)
     g.wait_ge(S.sent, sent[0])

@@ -5,25 +5,23 @@ TK = 512
 CW = TK // 2
 
 SCRATCH = {
-    "xq": ("sbuf", [128, TK], "bfloat16"),
     "w0": ("sbuf", [128, 256], "bfloat16"),
-    "xp": ("sbuf", [128, TK], "bfloat16"),
     "w1": ("sbuf", [128, 256], "bfloat16"),
     "wd2": ("sbuf", [128, 256], "bfloat16"),
     "wo": ("sbuf", [128, 256], "bfloat16"),
-    "so0": ("sbuf", [128, CW], "bfloat16"),
-    "so1": ("sbuf", [128, CW], "bfloat16"),
-    "sx0": ("sbuf", [128, CW], "bfloat16"),
-    "sx1": ("sbuf", [128, CW], "bfloat16"),
     "o1": ("sbuf", [128, TK], "bfloat16"),
     "o2": ("sbuf", [128, TK], "bfloat16"),
     "o3": ("sbuf", [128, TK], "bfloat16"),
     "zero": ("sbuf", [128, CW], "bfloat16"),
 }
+for _n in ("xq", "xp", "so", "sx"):
+    for _h in range(2):
+        SCRATCH["%s%d" % (_n, _h)] = ("sbuf", [128, CW], "bfloat16")
 for _b in range(8):
     SCRATCH["b%d" % _b] = ("psum", [128, 512], "float32")
 
-SEMAPHORES = ["ldx", "ldu", "ldw", "ldd", "arrA", "arrU", "arrX", "arrW", "arrD", "arrS0", "arrS1", "zs", "sent", "st"]
+SEMAPHORES = ["lda", "ldb", "ldu", "ldw", "ldd", "arrP", "arrQ", "arrU", "arrW", "arrD", "arrS0", "arrS1", "zs", "sent",
+              "st"]
 SEMAPHORES += ["m%d%d" % (s, k) for s in range(4) for k in range(4)]
 SEMAPHORES += ["v%d%d" % (s, k) for s in range(4) for k in range(4)]
 
@@ -41,6 +39,12 @@ def lanes(topo, src, cores, partner):
     return lo, (hi if hi else lo)
 
 
+def combs(topo, src, partner):
+    m = topo.mask(src, partner)
+    bits = [b for b in range(m.bit_length()) if (m >> b) & 1]
+    return sum(1 << b for b in bits[0::2]), sum(1 << b for b in bits[1::2])
+
+
 def rank_program(g, core, T, topo):
     rank = T.rank_of(core)
     if rank is None:
@@ -52,21 +56,27 @@ def rank_program(g, core, T, topo):
     mate = cores[rank ^ 1]
     far_even, far_odd = (cores[2], cores[3]) if top else (cores[0], cores[1])
     lo, hi = lanes(topo, core, cores, mate)
+    ca, cb = combs(topo, core, mate)
     mate_lo, mate_hi = lanes(topo, mate, cores, core)
+    mate_ca, mate_cb = combs(topo, mate, core)
     r0_lo, r0_hi = lanes(topo, cores[0], cores, cores[1])
     s_in = [count(lanes(topo, far_even, cores, far_odd)[0]), count(lanes(topo, far_odd, cores, far_even)[0])]
-    w1_in = {1: count(r0_hi), 3: count(r0_lo), 2: count(mate_lo)}.get(rank, 0)
+    w1_in = {1: count(r0_hi), 3: count(r0_lo), 2: count(mate_hi)}.get(rank, 0)
+    p_in = count(mate_ca)
+    q_in = count(mate_cb) if even else count(mate_hi)
     sent = [0]
 
     hs = 0 if even else 1
-    b0, b1 = hs * CW, (1 - hs) * CW
+    ho = 1 - hs
+    b0, b1 = hs * CW, ho * CW
     stages = [0, 1] + ([] if top else [2]) + ([] if even else [3])
     last = stages[-1]
     P = {0: [(b0, b0 + 128, 0, "v"), (b0 + 128, b0 + 192, 1, "s"), (b0 + 192, b0 + 256, 2, "v"), (b1, b1 + 256, 3, "s")]}
-    mid_banks = [(0, 3), (1, 2)]
+    mid_banks = [(0, 2), (1, 3)]
     for s in stages[1:-1]:
-        ba, bb = mid_banks.pop(0)
-        P[s] = [(0, 256, ba, "v"), (256, 512, bb, "v")]
+        bo, bx = mid_banks.pop(0)
+        bank = {hs: bo, ho: bx}
+        P[s] = [(0, 256, bank[0], "v"), (256, 512, bank[1], "v")]
     P[last] = [(0, 256, 4, "s"), (256, 384, 5, "v"), (384, 448, 6, "v"), (448, 512, 7, "s")]
 
     def halves(name):
@@ -84,8 +94,10 @@ def rank_program(g, core, T, topo):
                      dma_engine_mask=mask)
         sent[0] += count(mask)
 
-    def group(s, w, rhs, first, before=None):
+    def part(s, half, w, rhs, first, before=None):
         for k, (c0, c1, bank, _) in enumerate(P[s]):
+            if c0 // CW != half:
+                continue
             if before:
                 before(c0, c1)
             i = te.matmul(T["b%d" % bank][:, 0:c1 - c0], w, rhs(c0, c1), first, not first)
@@ -99,23 +111,26 @@ def rank_program(g, core, T, topo):
                     te.wait_ge(S["v%d%d" % (s, k)], 1)
         return f
 
+    mine = "xq" if even else "xp"
+    first_x, second_x = T["%s%d" % (mine, ho)], T["%s%d" % (mine, hs)]
+
     if even:
-        g.sync.dma_start(T.xq[:, :], T.x[:, :]).then_inc(S.ldx, 16)
-        g.scalar.dma_start(T.w0[:, :], T.wu[:, 0:256]).then_inc(S.ldu, 16)
-        if top:
-            g.scalar.dma_start(T.w1[:, :], T.wu[:, 256:512]).then_inc(S.ldw, 16)
-        else:
-            g.scalar.dma_start(T.wd2[:, :], T.wd[:, :]).then_inc(S.ldd, 16)
-    else:
-        g.sync.dma_start(T.xp[:, :], T.x[:, :]).then_inc(S.ldx, 16)
-        g.scalar.wait_ge(S.ldx, 16)
-        g.scalar.dma_start(T.wo[:, :], T.wd[:, :]).then_inc(S.ldd, 16)
+        g.sync.dma_start(T.w0[:, :], T.wu[:, 0:256]).then_inc(S.ldu, 16)
+    g.sync.dma_start(first_x[:, :], T.x[:, b1:b1 + CW]).then_inc(S.lda, 16)
+    if even and top:
+        g.sync.dma_start(T.w1[:, :], T.wu[:, 256:512]).then_inc(S.ldw, 16)
+    elif even:
+        g.sync.dma_start(T.wd2[:, :], T.wd[:, :]).then_inc(S.ldd, 16)
+    g.sync.dma_start(second_x[:, :], T.x[:, b0:b0 + CW]).then_inc(S.ldb, 16)
+    if not even:
+        g.sync.dma_start(T.wo[:, :], T.wd[:, :]).then_inc(S.ldd, 16)
 
     if even:
         g.wait_ge(S.ldu, 16)
-        send(mate, T.w0[:, :], T.w0[:, :], S.arrU, lo)
-        g.wait_ge(S.ldx, 16)
-        send(mate, T.xq[:, :], T.xq[:, :], S.arrA, hi)
+        send(mate, T.w0[:, :], T.w0[:, :], S.arrU, cb)
+    g.wait_ge(S.lda, 16)
+    send(mate, first_x[:, :], first_x[:, :], S.arrP, ca)
+    if even:
         if top:
             g.wait_ge(S.ldw, 16)
             rid3, pid3 = topo.addr(cores[3], core)
@@ -129,63 +144,94 @@ def rank_program(g, core, T, topo):
             sent[0] += count(lo) + count(hi)
         else:
             g.wait_ge(S.ldd, 16)
-            send(mate, T.wd2[:, :], T.wd2[:, :], S.arrD, hi)
+            send(mate, T.wd2[:, :], T.wd2[:, :], S.arrD, lo)
+        g.wait_ge(S.ldb, 16)
+        send(mate, second_x[:, :], second_x[:, :], S.arrQ, hi)
     else:
-        g.wait_ge(S.ldx, 16)
-        send(mate, T.xp[:, :], T.xp[:, :], S.arrX, lo)
-        if not top:
-            g.wait_ge(S.arrW, w1_in)
-            send(mate, T.w1[:, :], T.w1[:, :], S.arrW, lo)
+        g.wait_ge(S.ldb, 16)
+        send(mate, second_x[:, :], second_x[:, :], S.arrQ, cb)
     for k in range(3):
         g.wait_ge(S["v0%d" % k], 1)
     for dst in (far_odd, far_even):
         send(dst, T["sx%d" % hs][:, :], T["so%d" % hs][:, :], S["arrS%d" % hs], lo)
+    if rank == 3:
+        g.wait_ge(S.arrW, w1_in)
+        send(mate, T.w1[:, :], T.w1[:, :], S.arrW, hi)
 
     U0, V0 = T.w0[:, 0:128], T.w0[:, 128:256]
     U1, V1 = T.w1[:, 0:128], T.w1[:, 128:256]
-    te.wait_ge(S.ldx, 16)
+    W1near, W1far = (U1, V1) if top else (V1, U1)
+    D2, E2 = T.wd2[:, 0:128], T.wd2[:, 128:256]
+    xq, xp, so, sx = halves("xq"), halves("xp"), halves("so"), halves("sx")
+
+    def own_ready():
+        for k in range(3):
+            te.wait_ge(S["v0%d" % k], 1)
+
     if even:
         te.wait_ge(S.ldu, 16)
-        group(0, U0, whole("xq"), True)
-        te.wait_ge(S.arrX, count(mate_lo))
-        group(0, V0, whole("xp"), False)
-    else:
-        te.wait_ge(S.arrU, count(mate_lo))
-        group(0, V0, whole("xp"), True)
-        te.wait_ge(S.arrA, count(mate_hi))
-        group(0, U0, whole("xq"), False)
-        te.wait_ge(S.ldd, 16)
-        group(3, T.wo[:, 0:128], whole("xp"), True)
-    after(0)(0, TK)
-
-    def open1():
-        if rank == 0:
+        te.wait_ge(S.lda, 16)
+        part(0, ho, U0, xq, True)
+        te.wait_ge(S.ldb, 16)
+        part(0, hs, U0, xq, True)
+        te.wait_ge(S.arrP, p_in)
+        part(0, hs, V0, xp, False)
+        own_ready()
+        if top:
             te.wait_ge(S.ldw, 16)
+            part(1, hs, W1near, so, True)
         else:
-            te.wait_ge(S.arrW, w1_in)
-        group(1, U1 if top else V1, halves("so"), True)
-
-    def open2():
-        if even:
             te.wait_ge(S.ldd, 16)
+            part(2, hs, D2, so, True)
+        te.wait_ge(S.arrQ, q_in)
+        part(0, ho, V0, xp, False)
+        te.wait_ge(S.v03, 1)
+        if top:
+            part(1, ho, W1near, so, True)
         else:
-            te.wait_ge(S.arrD, count(mate_hi))
-        group(2, T.wd2[:, 0:128], halves("so"), True)
-
-    if top:
-        open1()
-    elif even:
-        open2()
-        open1()
+            part(2, ho, D2, so, True)
+            te.wait_ge(S.arrW, w1_in)
+            part(1, hs, W1near, so, True)
+            part(1, ho, W1near, so, True)
     else:
-        open1()
-        open2()
-    group(1, V1 if top else U1, halves("sx"), False, lambda c0, c1: te.wait_ge(S["arrS%d" % (c0 // CW)], s_in[c0 // CW]))
+        te.wait_ge(S.lda, 16)
+        te.wait_ge(S.ldb, 16)
+        te.wait_ge(S.ldd, 16)
+        part(3, 0, T.wo[:, 0:128], xp, True)
+        part(3, 1, T.wo[:, 0:128], xp, True)
+        te.wait_ge(S.arrU, count(mate_cb))
+        part(0, hs, V0, xp, True)
+        te.wait_ge(S.arrP, p_in)
+        part(0, hs, U0, xq, False)
+        part(0, ho, V0, xp, True)
+        own_ready()
+        if top:
+            te.wait_ge(S.arrW, w1_in)
+            part(1, hs, W1near, so, True)
+            te.wait_ge(S.arrQ, q_in)
+            part(0, ho, U0, xq, False)
+            te.wait_ge(S.v03, 1)
+            part(1, ho, W1near, so, True)
+        else:
+            te.wait_ge(S.arrD, count(mate_lo))
+            part(2, hs, D2, so, True)
+            te.wait_ge(S.arrQ, q_in)
+            part(0, ho, U0, xq, False)
+            te.wait_ge(S.v03, 1)
+            part(2, ho, D2, so, True)
+            te.wait_ge(S.arrW, w1_in)
+            part(1, hs, W1near, so, True)
+            part(1, ho, W1near, so, True)
+
+    for h in range(2):
+        part(1, h, W1far, sx, False, lambda c0, c1: te.wait_ge(S["arrS%d" % (c0 // CW)], s_in[c0 // CW]))
     if not top:
-        group(2, T.wd2[:, 128:256], whole("o1"), False, after(1))
+        for h in range(2):
+            part(2, h, E2, whole("o1"), False, after(1))
     if not even:
         prev = stages[-2]
-        group(3, T.wo[:, 128:256], whole("o%d" % prev), False, after(prev))
+        for h in range(2):
+            part(3, h, T.wo[:, 128:256], whole("o%d" % prev), False, after(prev))
 
     ve.memset(T.zero[:, :], 0.0).then_inc(S.zs, 1)
     ve.wait_ge(S.zs, 1)

from concourse.bass import DstId, RemoteDMATransfer
from concourse.mybir import AluOpType, ActivationFunctionType

TK = 512
CW = TK // 2

SCRATCH = {
    "w0": ("sbuf", [128, 256], "bfloat16"),
    "w1": ("sbuf", [128, 256], "bfloat16"),
    "wd2": ("sbuf", [128, 256], "bfloat16"),
    "wo": ("sbuf", [128, 256], "bfloat16"),
    "o1": ("sbuf", [128, TK], "bfloat16"),
    "o2": ("sbuf", [128, TK], "bfloat16"),
    "o3": ("sbuf", [128, TK], "bfloat16"),
    "zero": ("sbuf", [128, CW], "bfloat16"),
}
for _n in ("xq", "xp", "so", "sx"):
    for _h in range(2):
        SCRATCH["%s%d" % (_n, _h)] = ("sbuf", [128, CW], "bfloat16")
for _b in range(8):
    SCRATCH["b%d" % _b] = ("psum", [128, 512], "float32")

SEMAPHORES = ["lda", "ldb", "ldu", "ldw", "ldd", "arrP", "arrQ", "arrU", "arrW", "arrD", "arrS0", "arrS1", "zs", "sent",
              "st"]
SEMAPHORES += ["m%d%d" % (s, k) for s in range(4) for k in range(4)]
SEMAPHORES += ["v%d%d" % (s, k) for s in range(4) for k in range(4)]


def count(mask):
    return bin(mask).count("1")


def lanes(topo, src, cores, partner):
    lo = topo.mask(src, partner)
    for d in cores:
        if d != src:
            lo &= topo.mask(src, d)
    hi = topo.mask(src, partner) & ~lo
    return lo, (hi if hi else lo)


def combs(topo, src, partner):
    m = topo.mask(src, partner)
    bits = [b for b in range(m.bit_length()) if (m >> b) & 1]
    return sum(1 << b for b in bits[0::2]), sum(1 << b for b in bits[1::2])


def rank_program(g, core, T, topo):
    rank = T.rank_of(core)
    if rank is None:
        return
    S, cores = T.sem, T.cores
    te, ve, ac = g.tensor, g.vector, g.scalar
    even = rank % 2 == 0
    top = rank < 2
    mate = cores[rank ^ 1]
    far_even, far_odd = (cores[2], cores[3]) if top else (cores[0], cores[1])
    lo, hi = lanes(topo, core, cores, mate)
    ca, cb = combs(topo, core, mate)
    mate_lo, mate_hi = lanes(topo, mate, cores, core)
    mate_ca, mate_cb = combs(topo, mate, core)
    r0_lo, r0_hi = lanes(topo, cores[0], cores, cores[1])
    s_in = [count(lanes(topo, far_even, cores, far_odd)[0]), count(lanes(topo, far_odd, cores, far_even)[0])]
    w1_in = {1: count(r0_hi), 3: count(r0_lo), 2: count(mate_hi)}.get(rank, 0)
    p_in = count(mate_ca)
    q_in = count(mate_cb) if even else count(mate_hi)
    sent = [0]

    hs = 0 if even else 1
    ho = 1 - hs
    b0, b1 = hs * CW, ho * CW
    stages = [0, 1] + ([] if top else [2]) + ([] if even else [3])
    last = stages[-1]
    P = {0: [(b0, b0 + 128, 0, "v"), (b0 + 128, b0 + 192, 1, "s"), (b0 + 192, b0 + 256, 2, "v"), (b1, b1 + 256, 3, "s")]}
    mid_banks = [(0, 2), (1, 3)]
    for s in stages[1:-1]:
        bo, bx = mid_banks.pop(0)
        bank = {hs: bo, ho: bx}
        P[s] = [(0, 256, bank[0], "v"), (256, 512, bank[1], "v")]
    P[last] = [(0, 256, 4, "s"), (256, 384, 5, "v"), (384, 448, 6, "v"), (448, 512, 7, "s")]

    def halves(name):
        return lambda c0, c1: T["%s%d" % (name, c0 // CW)][:, c0 % CW:c0 % CW + (c1 - c0)]

    def whole(name):
        return lambda c0, c1: T[name][:, c0:c1]

    def outbuf(s):
        return halves("so") if s == 0 else whole("o%d" % s)

    def send(dst, buf_out, buf_in, sem, mask):
        rid, pid = topo.addr(dst, core)
        g.remote_dma(out_ap=buf_out, in_ap=buf_in, remote_sem=sem, local_sem=S.sent, pid=pid, routing_id=rid,
                     dma_engine_mask=mask)
        sent[0] += count(mask)

    def part(s, half, w, rhs, first, before=None):
        for k, (c0, c1, bank, _) in enumerate(P[s]):
            if c0 // CW != half:
                continue
            if before:
                before(c0, c1)
            i = te.matmul(T["b%d" % bank][:, 0:c1 - c0], w, rhs(c0, c1), first, not first)
            if not first:
                i.then_inc(S["m%d%d" % (s, k)], 1)

    def after(s):
        def f(c0, c1):
            for k, (d0, d1, _, _) in enumerate(P[s]):
                if d0 < c1 and c0 < d1:
                    te.wait_ge(S["v%d%d" % (s, k)], 1)
        return f

    mine = "xq" if even else "xp"
    first_x, second_x = T["%s%d" % (mine, ho)], T["%s%d" % (mine, hs)]

    if even:
        g.sync.dma_start(T.w0[:, :], T.wu[:, 0:256]).then_inc(S.ldu, 16)
    g.sync.dma_start(first_x[:, :], T.x[:, b1:b1 + CW]).then_inc(S.lda, 16)
    if even and top:
        g.sync.dma_start(T.w1[:, :], T.wu[:, 256:512]).then_inc(S.ldw, 16)
    elif even:
        g.sync.dma_start(T.wd2[:, :], T.wd[:, :]).then_inc(S.ldd, 16)
    g.sync.dma_start(second_x[:, :], T.x[:, b0:b0 + CW]).then_inc(S.ldb, 16)
    if not even:
        g.sync.dma_start(T.wo[:, :], T.wd[:, :]).then_inc(S.ldd, 16)

    if even:
        g.wait_ge(S.ldu, 16)
        send(mate, T.w0[:, :], T.w0[:, :], S.arrU, cb)
    g.wait_ge(S.lda, 16)
    send(mate, first_x[:, :], first_x[:, :], S.arrP, ca)
    if even:
        if top:
            g.wait_ge(S.ldw, 16)
            rid3, pid3 = topo.addr(cores[3], core)
            rid1, pid1 = topo.addr(mate, core)
            g.remote_dma_fused([
                RemoteDMATransfer(dst_ids=[DstId(rid=rid3, pnc=pid3)], dma_engine_mask=lo, remote_sem=S.arrW,
                                  srcs=[T.w1[:, :]], dsts=[T.w1[:, :]]),
                RemoteDMATransfer(dst_ids=[DstId(rid=rid1, pnc=pid1)], dma_engine_mask=hi, remote_sem=S.arrW,
                                  srcs=[T.w1[:, :]], dsts=[T.w1[:, :]]),
            ], local_sem=S.sent)
            sent[0] += count(lo) + count(hi)
        else:
            g.wait_ge(S.ldd, 16)
            send(mate, T.wd2[:, :], T.wd2[:, :], S.arrD, lo)
        g.wait_ge(S.ldb, 16)
        send(mate, second_x[:, :], second_x[:, :], S.arrQ, hi)
    else:
        g.wait_ge(S.ldb, 16)
        send(mate, second_x[:, :], second_x[:, :], S.arrQ, cb)
    for k in range(3):
        g.wait_ge(S["v0%d" % k], 1)
    for dst in (far_odd, far_even):
        send(dst, T["sx%d" % hs][:, :], T["so%d" % hs][:, :], S["arrS%d" % hs], lo)
    if rank == 3:
        g.wait_ge(S.arrW, w1_in)
        send(mate, T.w1[:, :], T.w1[:, :], S.arrW, hi)

    U0, V0 = T.w0[:, 0:128], T.w0[:, 128:256]
    U1, V1 = T.w1[:, 0:128], T.w1[:, 128:256]
    W1near, W1far = (U1, V1) if top else (V1, U1)
    D2, E2 = T.wd2[:, 0:128], T.wd2[:, 128:256]
    xq, xp, so, sx = halves("xq"), halves("xp"), halves("so"), halves("sx")

    def own_ready():
        for k in range(3):
            te.wait_ge(S["v0%d" % k], 1)

    if even:
        te.wait_ge(S.ldu, 16)
        te.wait_ge(S.lda, 16)
        part(0, ho, U0, xq, True)
        te.wait_ge(S.ldb, 16)
        part(0, hs, U0, xq, True)
        te.wait_ge(S.arrP, p_in)
        part(0, hs, V0, xp, False)
        own_ready()
        if top:
            te.wait_ge(S.ldw, 16)
            part(1, hs, W1near, so, True)
        else:
            te.wait_ge(S.ldd, 16)
            part(2, hs, D2, so, True)
        te.wait_ge(S.arrQ, q_in)
        part(0, ho, V0, xp, False)
        te.wait_ge(S.v03, 1)
        if top:
            part(1, ho, W1near, so, True)
        else:
            part(2, ho, D2, so, True)
            te.wait_ge(S.arrW, w1_in)
            part(1, hs, W1near, so, True)
            part(1, ho, W1near, so, True)
    else:
        te.wait_ge(S.lda, 16)
        te.wait_ge(S.ldb, 16)
        te.wait_ge(S.ldd, 16)
        part(3, 0, T.wo[:, 0:128], xp, True)
        part(3, 1, T.wo[:, 0:128], xp, True)
        te.wait_ge(S.arrU, count(mate_cb))
        part(0, hs, V0, xp, True)
        te.wait_ge(S.arrP, p_in)
        part(0, hs, U0, xq, False)
        part(0, ho, V0, xp, True)
        own_ready()
        if top:
            te.wait_ge(S.arrW, w1_in)
            part(1, hs, W1near, so, True)
            te.wait_ge(S.arrQ, q_in)
            part(0, ho, U0, xq, False)
            te.wait_ge(S.v03, 1)
            part(1, ho, W1near, so, True)
        else:
            te.wait_ge(S.arrD, count(mate_lo))
            part(2, hs, D2, so, True)
            te.wait_ge(S.arrQ, q_in)
            part(0, ho, U0, xq, False)
            te.wait_ge(S.v03, 1)
            part(2, ho, D2, so, True)
            te.wait_ge(S.arrW, w1_in)
            part(1, hs, W1near, so, True)
            part(1, ho, W1near, so, True)

    for h in range(2):
        part(1, h, W1far, sx, False, lambda c0, c1: te.wait_ge(S["arrS%d" % (c0 // CW)], s_in[c0 // CW]))
    if not top:
        for h in range(2):
            part(2, h, E2, whole("o1"), False, after(1))
    if not even:
        prev = stages[-2]
        for h in range(2):
            part(3, h, T.wo[:, 128:256], whole("o%d" % prev), False, after(prev))

    ve.memset(T.zero[:, :], 0.0).then_inc(S.zs, 1)
    ve.wait_ge(S.zs, 1)
    for s in stages:
        for k, (c0, c1, bank, eng) in enumerate(P[s]):
            acc, out = T["b%d" % bank][:, 0:c1 - c0], outbuf(s)(c0, c1)
            if eng == "v":
                ve.wait_ge(S["m%d%d" % (s, k)], 1)
                ve.tensor_tensor(out, acc, T.zero[:, 0:c1 - c0], AluOpType.max).then_inc(S["v%d%d" % (s, k)], 1)
            else:
                ac.wait_ge(S["m%d%d" % (s, k)], 1)
                ac.activation(out, acc, ActivationFunctionType.Relu).then_inc(S["v%d%d" % (s, k)], 1)

    for k in range(len(P[last])):
        g.sync.wait_ge(S["v%d%d" % (last, k)], 1)
    g.sync.dma_start(T.y[:, :], T["o%d" % last][:, :]).then_inc(S.st, 16)
    g.sync.wait_ge(S.st, 16)
    g.wait_ge(S.sent, sent[0])
